import numpy as np
import ml_dtypes


def mxq(x, axis, fmt="e4m3"):
    dtype, down = {"e4m3": (ml_dtypes.float8_e4m3fn, 7), "e5m2": (ml_dtypes.float8_e5m2, 14)}[fmt]
    v = np.moveaxis(np.asarray(x, np.float32).astype(ml_dtypes.bfloat16).astype(np.float64), axis, -1)
    blocks = v.reshape(v.shape[:-1] + (-1, 32))
    amax = np.abs(blocks).max(-1, keepdims=True)
    byte = np.maximum(np.where(amax > 0, np.frexp(amax)[1] - 1 + 127, 0) - down, 1)
    scale = np.exp2(byte - 127.0)
    codes = (blocks / scale).astype(np.float32).astype(dtype).astype(np.float64)
    return np.moveaxis((codes * scale).reshape(v.shape), -1, axis)


WIDE = False


def mx_kscale(k):
    if not WIDE:
        return np.ones(k)
    levels = np.array([10, -10, 5, -5, 0])
    if k % 512:
        return np.exp2(np.random.permutation(np.resize(levels, k // 32))).repeat(32)
    a = np.empty((k // 512, 16))
    for p in range(k // 512):
        a[p, :8] = np.random.permutation(np.resize(levels, 8))
        for g in range(8):
            far = levels[np.abs(levels - a[p, g]) >= 10]
            a[p, g + 8] = far[np.random.randint(len(far))]
    return np.exp2(a.ravel()).repeat(32)


def f64(x):
    return np.asarray(x).astype(np.float64)


def striped(idx):
    return np.tile(idx.reshape(-1, 16).T, (8, 1)).astype(np.uint16)


def unstriped(offs):
    return offs[:16].T.reshape(-1).astype(np.int64)


def gelu(v):
    return 0.5 * v * (1.0 + np.tanh(np.sqrt(2.0 / np.pi) * (v + 0.044715 * v**3)))


K, T, E, C, H, N = 512, 512, 4, 256, 1024, 256


def by_expert(wq, xq):
    return np.concatenate([wq[e].T @ xq[:, e * C:(e + 1) * C] for e in range(E)], axis=1)


def setup_inputs():
    n = np.random.standard_normal
    s = mx_kscale(K)[:, None]
    u = mx_kscale(H)
    first = np.random.permutation(np.repeat(np.arange(E), T // E))
    second = (first + 1 + np.random.permutation(np.repeat(np.arange(E - 1), -(-T // (E - 1)))[:T])) % E
    while np.bincount(second, minlength=E).max() != T // E:
        load = np.bincount(second, minlength=E); hi, lo = int(load.argmax()), int(load.argmin())
        t = np.flatnonzero((second == hi) & (first != lo))[0]; second[t] = lo
    slot_token = np.empty(E * C, np.int64); pos = np.empty((2, T), np.int64); fill = np.zeros(E, np.int64)
    place = np.stack([np.random.permutation(C) for _ in range(E)])
    for r, deal in enumerate((first, second)):
        for t in np.random.permutation(T):
            e = deal[t]; j = e * C + place[e, fill[e]]; fill[e] += 1; slot_token[j] = t; pos[r, t] = j
    g = np.random.uniform(0.2, 0.8, T)
    return {
        "xT": (n((K, T)) * s).astype(np.float32),
        "w1": (n((E, K, H)) / np.sqrt(K) / s[None]).astype(np.float32),
        "w3": (n((E, K, H)) / np.sqrt(K) / s[None] * u[None, None, :]).astype(np.float32),
        "w2": (n((E, H, N)) / np.sqrt(H) / u[None, :, None]).astype(np.float32),
        "gate": np.stack([np.tile(g, (N, 1)), np.tile(1.0 - g, (N, 1))]).astype(np.float32),
        "offs": striped(slot_token),
        "pos1": striped(pos[0]),
        "pos2": striped(pos[1]),
    }


def reference(xT, w1, w3, w2, gate, offs, pos1, pos2):
    idx = unstriped(offs)
    xq = mxq(f64(xT)[:, idx], 0, "e4m3")
    h = gelu(by_expert(mxq(f64(w1), 1, "e4m3"), xq))
    h = h * by_expert(mxq(f64(w3), 1, "e4m3"), xq)
    y = by_expert(mxq(f64(w2), 1, "e4m3"), mxq(h, 0, "e4m3"))
    return f64(gate[0]) * y[:, unstriped(pos1)] + f64(gate[1]) * y[:, unstriped(pos2)]

@@ -1,0 +1,253 @@
+from contextlib import ExitStack
+
+import concourse.mybir as mybir
+
+FLOPS = 2 * 1024 * (2 * 512 * 1024 + 1024 * 256)
+
+K, T, E, C, H, N = 512, 512, 4, 256, 1024, 256
+P = 128
+PACK = 4
+PASS = P * PACK
+G = H // PASS
+HALF = 128
+M_TILES = N // P
+
+F32 = mybir.dt.float32
+BF16 = mybir.dt.bfloat16
+U32 = mybir.dt.uint32
+U16 = mybir.dt.uint16
+U8 = mybir.dt.uint8
+FP8X4 = mybir.dt.float8_e4m3fn_x4
+GELU = mybir.ActivationFunctionType.Gelu_apprx_tanh
+MULT = mybir.AluOpType.mult
+ADD = mybir.AluOpType.add
+
+WHO_W1 = (("A", "A"),) * 4
+WHO_W3 = (("A", "A"),) * 4
+WHO_W2 = (("A", "A"), ("A", "A"), ("A", "A"), ("V", "V"))
+LOOK = 4
+
+
+def cast(nc, who, out, in_):
+    if who == "A":
+        nc.any.tensor_copy(out=out, in_=in_)
+    elif who == "V":
+        nc.vector.tensor_copy(out=out, in_=in_)
+    else:
+        nc.scalar.copy(out=out, in_=in_)
+
+
+def tile_routed_moe_kernel(tc, xT, w1, w3, w2, gate, offs, pos1, pos2, out):
+    nc = tc.nc
+    with ExitStack() as ctx:
+        lists = ctx.enter_context(tc.tile_pool(name="lists", bufs=1))
+        keep = ctx.enter_context(tc.tile_pool(name="keep", bufs=1))
+        raw = ctx.enter_context(tc.tile_pool(name="raw", bufs=LOOK + 1))
+        stage = ctx.enter_context(tc.tile_pool(name="stage", bufs=3))
+        work = ctx.enter_context(tc.tile_pool(name="work", bufs=3))
+        psum = ctx.enter_context(tc.psum_pool(name="psum", bufs=3))
+        psum_y = ctx.enter_context(tc.psum_pool(name="psum_y", bufs=2))
+
+        offs_t = lists.tile([P, E * C // 16], U16, name="offs_t")
+        pos1_t = lists.tile([P, T // 16], U16, name="pos1_t")
+        pos2_t = lists.tile([P, T // 16], U16, name="pos2_t")
+        nc.sync.dma_start(offs_t[:], offs)
+
+        warm = keep.tile([P, 1], F32, name="warm")
+        warm_out = keep.tile([P, 1], F32, name="warm_out")
+        nc.vector.memset(warm[:], 0.0)
+        nc.scalar.activation(out=warm_out[:], in_=warm[:], func=GELU)
+
+        xq = keep.tile([P, T], U32, name="xq", align_bytes=64)
+        xs = keep.tile([P, T], U8, name="xs", align_bytes=64)
+        xg_w = keep.tile([P, E * C], U32, name="xg_w", align_bytes=64)
+        xg_s = keep.tile([P, E * C], U8, name="xg_s", align_bytes=64)
+        nc.gpsimd.memset(xs[:], 0)
+
+        w1q = [keep.tile([P, H], U32, name="w1q%d" % e, align_bytes=64) for e in range(E)]
+        w1s = [keep.tile([P, H], U8, name="w1s%d" % e, align_bytes=64) for e in range(E)]
+        w3q = [keep.tile([P, H], U32, name="w3q%d" % e, align_bytes=64) for e in range(E)]
+        w3s = [keep.tile([P, H], U8, name="w3s%d" % e, align_bytes=64) for e in range(E)]
+        w2q = [keep.tile([P, G * N], U32, name="w2q%d" % e, align_bytes=64) for e in range(E)]
+        w2s = [keep.tile([P, G * N], U8, name="w2s%d" % e, align_bytes=64) for e in range(E)]
+        hq = [keep.tile([P, G * C], U32, name="hq%d" % e, align_bytes=64) for e in range(E)]
+        hs = [keep.tile([P, G * C], U8, name="hs%d" % e, align_bytes=64) for e in range(E)]
+        y_sb = [keep.tile([P, E * C], F32, name="y_sb%d" % m) for m in range(M_TILES)]
+        gate_t = [[keep.tile([P, T], F32, name="gate%d_%d" % (r, m)) for m in range(M_TILES)] for r in range(2)]
+
+        plan = [("x", 0)]
+        for e in range(E):
+            plan.append(("w1", e))
+            plan.append(("w3", e))
+        for e in range(E):
+            plan.append(("w2", e))
+        loaded = {}
+
+        def issue(i):
+            if i >= len(plan):
+                return
+            kind, e = plan[i]
+            if kind == "x":
+                t = raw.tile([P, PACK, T], F32, name="x_raw", tag="raw")
+                nc.sync.dma_start(out=t[:], in_=xT.rearrange("(p j) t -> p j t", j=PACK))
+            elif kind == "w2":
+                t = raw.tile([P, G, PACK, N], F32, name="w2_raw", tag="raw")
+                if e < E - 1:
+                    nc.sync.dma_start(out=t[:], in_=w2[e].rearrange("(g p j) n -> p g j n", g=G, j=PACK))
+                else:
+                    for g in range(G):
+                        nc.sync.dma_start(out=t[:, g], in_=w2[e, g * PASS:(g + 1) * PASS, :].rearrange("(p j) n -> p j n", j=PACK))
+            else:
+                src = w1 if kind == "w1" else w3
+                t = raw.tile([P, PACK, H], F32, name="w13_raw", tag="raw")
+                nc.sync.dma_start(out=t[:], in_=src[e].rearrange("(p j) h -> p j h", j=PACK))
+            loaded[(kind, e)] = t
+            if i == len(plan) - 1:
+                for m in range(M_TILES):
+                    for r in range(2):
+                        nc.sync.dma_start(out=gate_t[r][m][:], in_=gate[r, m * P:(m + 1) * P, :])
+
+        issue(0)
+        nc.sync.dma_start(pos1_t[:], pos1)
+        nc.sync.dma_start(pos2_t[:], pos2)
+        for i in range(1, LOOK + 1):
+            issue(i)
+        step = [LOOK + 1]
+
+        def next_load():
+            issue(step[0])
+            step[0] += 1
+
+        x_raw = loaded[("x", 0)]
+        xb = stage.tile([P, T * PACK], BF16, name="xb", tag="grouped", align_bytes=64)
+        for half, who in enumerate(("V", "S")):
+            cast(
+                nc,
+                who,
+                out=xb[:, half * 1024:(half + 1) * 1024].rearrange("p (c i j) -> p c j i", i=4, j=PACK),
+                in_=x_raw[:, :, half * 256:(half + 1) * 256].rearrange("p j (c i) -> p c j i", i=4),
+            )
+        nc.vector.quantize_mx(out=xq[:].bitcast(FP8X4), scales=xs[:], in_=xb[:])
+
+        def gather(e):
+            lst = offs_t[:, e * (C // 16):(e + 1) * (C // 16)]
+            nc.vector.tensor_copy(out=xg_w[:, e * C:(e + 1) * C], in_=xq[:].indirect(lst))
+            nc.vector.tensor_copy(out=xg_s[:, e * C:(e + 1) * C], in_=xs[:].indirect(lst))
+
+        gather(0)
+
+        def prep_w13(t_raw, codes, scales, who):
+            grouped = stage.tile([P, H * PACK], BF16, name="grouped", tag="grouped", align_bytes=64)
+            for g in range(G):
+                cast(
+                    nc,
+                    who[g],
+                    out=grouped[:, g * PASS * PACK:(g + 1) * PASS * PACK].rearrange("p (t m j) -> p m j t", t=PACK, j=PACK),
+                    in_=t_raw[:, :, g * PASS:(g + 1) * PASS].rearrange("p j (m t) -> p m j t", t=PACK),
+                )
+            nc.vector.quantize_mx(out=codes[:].bitcast(FP8X4), scales=scales[:], in_=grouped[:])
+
+        def prep_w2(t_raw, codes, scales, who, split):
+            grouped = stage.tile([P, G * N * PACK], BF16, name="grouped2", tag="grouped", align_bytes=64)
+            for g in range(G):
+                cast(
+                    nc,
+                    who[g],
+                    out=grouped[:, g * N * PACK:(g + 1) * N * PACK].rearrange("p (c i j) -> p c j i", i=4, j=PACK),
+                    in_=t_raw[:, g, :, :].rearrange("p j (c i) -> p c j i", i=4),
+                )
+                if split:
+                    wc = slice(g * N, (g + 1) * N)
+                    nc.vector.quantize_mx(
+                        out=codes[:, wc].bitcast(FP8X4), scales=scales[:, wc], in_=grouped[:, g * N * PACK:(g + 1) * N * PACK]
+                    )
+            if not split:
+                nc.vector.quantize_mx(out=codes[:].bitcast(FP8X4), scales=scales[:], in_=grouped[:])
+
+        def layer1(e, g):
+            hb = work.tile([P, C * PACK], BF16, name="hb", tag="hb", align_bytes=64)
+            ga = work.tile([P, PACK, C], F32, name="ga", tag="ga")
+            for u in range(2):
+                pa = psum.tile([P, 2, C], F32, name="pa", tag="pa")
+                for v in range(2):
+                    t = 2 * u + v
+                    wc = slice(g * PASS + t * P, g * PASS + (t + 1) * P)
+                    nc.tensor.matmul_mx(
+                        out=pa[:, v, :],
+                        lhsT=w1q[e][:, wc].bitcast(FP8X4),
+                        lhsT_scale=w1s[e][:, wc],
+                        rhs=xg_w[:, e * C:(e + 1) * C].bitcast(FP8X4),
+                        rhs_scale=xg_s[:, e * C:(e + 1) * C],
+                        start=True,
+                        stop=True,
+                    )
+                nc.scalar.activation(out=ga[:, 2 * u:2 * u + 2, :], in_=pa[:], func=GELU)
+            for s in range(C // HALF):
+                cols = slice(e * C + s * HALF, e * C + (s + 1) * HALF)
+                pb = psum.tile([P, PACK, HALF], F32, name="pb", tag="pb")
+                for t in range(PACK):
+                    wc = slice(g * PASS + t * P, g * PASS + (t + 1) * P)
+                    nc.tensor.matmul_mx(
+                        out=pb[:, t, :],
+                        lhsT=w3q[e][:, wc].bitcast(FP8X4),
+                        lhsT_scale=w3s[e][:, wc],
+                        rhs=xg_w[:, cols].bitcast(FP8X4),
+                        rhs_scale=xg_s[:, cols],
+                        start=True,
+                        stop=True,
+                    )
+                nc.vector.tensor_tensor(
+                    out=hb[:, s * HALF * PACK:(s + 1) * HALF * PACK].rearrange("p (n j) -> p n j", j=PACK),
+                    in0=ga[:, :, s * HALF:(s + 1) * HALF].rearrange("p j n -> p n j"),
+                    in1=pb[:].rearrange("p j n -> p n j"),
+                    op=MULT,
+                )
+            hc = slice(g * C, (g + 1) * C)
+            nc.vector.quantize_mx(out=hq[e][:, hc].bitcast(FP8X4), scales=hs[e][:, hc], in_=hb[:])
+
+        def layer2(e):
+            if e < E - 1:
+                py = psum_y.tile([P, M_TILES, C], F32, name="py", tag="py")
+                acc = [py[:, m, :] for m in range(M_TILES)]
+                order = [(m, g) for m in range(M_TILES) for g in range(G)]
+            else:
+                acc = [psum_y.tile([P, C], F32, name="py%d" % m, tag="py")[:] for m in range(M_TILES)]
+                order = [(m, g) for g in range(G) for m in range(M_TILES)]
+            for m, g in order:
+                if True:
+                    wc = slice(g * N + m * P, g * N + (m + 1) * P)
+                    hc = slice(g * C, (g + 1) * C)
+                    nc.tensor.matmul_mx(
+                        out=acc[m],
+                        lhsT=w2q[e][:, wc].bitcast(FP8X4),
+                        lhsT_scale=w2s[e][:, wc],
+                        rhs=hq[e][:, hc].bitcast(FP8X4),
+                        rhs_scale=hs[e][:, hc],
+                        start=(g == 0),
+                        stop=(g == G - 1),
+                    )
+            for m in range(M_TILES):
+                nc.scalar.copy(out=y_sb[m][:, e * C:(e + 1) * C], in_=acc[m])
+
+        for e in range(E):
+            prep_w13(loaded[("w1", e)], w1q[e], w1s[e], WHO_W1[e])
+            next_load()
+            prep_w13(loaded[("w3", e)], w3q[e], w3s[e], WHO_W3[e])
+            next_load()
+            if e > 0:
+                gather(e)
+            for g in range(G):
+                layer1(e, g)
+        for e in range(E):
+            prep_w2(loaded[("w2", e)], w2q[e], w2s[e], WHO_W2[e], e == E - 1)
+            next_load()
+            layer2(e)
+
+        for m in range(M_TILES):
+            o1 = work.tile([P, T], F32, name="o1", tag="o1")
+            o2 = work.tile([P, T], F32, name="o2", tag="o2")
+            o = work.tile([P, T], F32, name="o", tag="o")
+            nc.vector.tensor_tensor(out=o1[:], in0=y_sb[m][:].indirect(pos1_t[:]), in1=gate_t[0][m][:], op=MULT)
+            nc.vector.tensor_tensor(out=o2[:], in0=y_sb[m][:].indirect(pos2_t[:]), in1=gate_t[1][m][:], op=MULT)
+            nc.vector.tensor_tensor(out=o[:], in0=o1[:], in1=o2[:], op=ADD)
+            nc.sync.dma_start(out=out[m * P:(m + 1) * P, :], in_=o[:])

@@ -15,6 +15,7 @@ M_TILES = N // P
 F32 = mybir.dt.float32
 BF16 = mybir.dt.bfloat16
 U32 = mybir.dt.uint32
+I32 = mybir.dt.int32
 U16 = mybir.dt.uint16
 U8 = mybir.dt.uint8
 FP8X4 = mybir.dt.float8_e4m3fn_x4
@@ -26,6 +27,7 @@ WHO_W1 = (("A", "A"),) * 4
 WHO_W3 = (("A", "A"),) * 4
 WHO_W2 = (("A", "A"), ("A", "A"), ("A", "A"), ("V", "V"))
 LOOK = 4
+WINDOW = 2 * E * C
 
 
 def cast(nc, who, out, in_):
@@ -58,11 +60,12 @@ def tile_routed_moe_kernel(tc, xT, w1, w3, w2, gate, offs, pos1, pos2, out):
         nc.vector.memset(warm[:], 0.0)
         nc.scalar.activation(out=warm_out[:], in_=warm[:], func=GELU)
 
-        xq = keep.tile([P, T], U32, name="xq", align_bytes=64)
-        xs = keep.tile([P, T], U8, name="xs", align_bytes=64)
+        xq = keep.tile([P, WINDOW], I32, name="xq", align_bytes=64)
+        xs = keep.tile([P, WINDOW], U8, name="xs", align_bytes=64)
         xg_w = keep.tile([P, E * C], U32, name="xg_w", align_bytes=64)
         xg_s = keep.tile([P, E * C], U8, name="xg_s", align_bytes=64)
         nc.gpsimd.memset(xs[:], 0)
+        nc.vector.memset(xq[:, T:], 0)
 
         w1q = [keep.tile([P, H], U32, name="w1q%d" % e, align_bytes=64) for e in range(E)]
         w1s = [keep.tile([P, H], U8, name="w1s%d" % e, align_bytes=64) for e in range(E)]
@@ -76,7 +79,10 @@ def tile_routed_moe_kernel(tc, xT, w1, w3, w2, gate, offs, pos1, pos2, out):
         gate_t = [[keep.tile([P, T], F32, name="gate%d_%d" % (r, m)) for m in range(M_TILES)] for r in range(2)]
 
         plan = [("x", 0)]
-        for e in range(E):
+        for g in range(G):
+            plan.append(("w1h%d" % g, 0))
+            plan.append(("w3h%d" % g, 0))
+        for e in range(1, E):
             plan.append(("w1", e))
             plan.append(("w3", e))
         for e in range(E):
@@ -97,6 +103,11 @@ def tile_routed_moe_kernel(tc, xT, w1, w3, w2, gate, offs, pos1, pos2, out):
                 else:
                     for g in range(G):
                         nc.sync.dma_start(out=t[:, g], in_=w2[e, g * PASS:(g + 1) * PASS, :].rearrange("(p j) n -> p j n", j=PACK))
+            elif len(kind) == 4:
+                src = w1 if kind[:2] == "w1" else w3
+                g = int(kind[3])
+                t = raw.tile([P, PACK, PASS], F32, name="w13h_raw", tag="raw")
+                nc.sync.dma_start(out=t[:], in_=src[e, :, g * PASS:(g + 1) * PASS].rearrange("(p j) h -> p j h", j=PACK))
             else:
                 src = w1 if kind == "w1" else w3
                 t = raw.tile([P, PACK, H], F32, name="w13_raw", tag="raw")
@@ -127,14 +138,9 @@ def tile_routed_moe_kernel(tc, xT, w1, w3, w2, gate, offs, pos1, pos2, out):
                 out=xb[:, half * 1024:(half + 1) * 1024].rearrange("p (c i j) -> p c j i", i=4, j=PACK),
                 in_=x_raw[:, :, half * 256:(half + 1) * 256].rearrange("p j (c i) -> p c j i", i=4),
             )
-        nc.vector.quantize_mx(out=xq[:].bitcast(FP8X4), scales=xs[:], in_=xb[:])
-
-        def gather(e):
-            lst = offs_t[:, e * (C // 16):(e + 1) * (C // 16)]
-            nc.vector.tensor_copy(out=xg_w[:, e * C:(e + 1) * C], in_=xq[:].indirect(lst))
-            nc.vector.tensor_copy(out=xg_s[:, e * C:(e + 1) * C], in_=xs[:].indirect(lst))
-
-        gather(0)
+        nc.vector.quantize_mx(out=xq[:, 0:T].bitcast(FP8X4), scales=xs[:, 0:T], in_=xb[:])
+        nc.vector.tensor_copy(out=xg_w[:], in_=xq[:].bitcast(U32).indirect(offs_t[:]))
+        nc.vector.tensor_copy(out=xg_s[:], in_=xs[:].indirect(offs_t[:]))
 
         def prep_w13(t_raw, codes, scales, who):
             grouped = stage.tile([P, H * PACK], BF16, name="grouped", tag="grouped", align_bytes=64)
@@ -146,6 +152,17 @@ def tile_routed_moe_kernel(tc, xT, w1, w3, w2, gate, offs, pos1, pos2, out):
                     in_=t_raw[:, :, g * PASS:(g + 1) * PASS].rearrange("p j (m t) -> p m j t", t=PACK),
                 )
             nc.vector.quantize_mx(out=codes[:].bitcast(FP8X4), scales=scales[:], in_=grouped[:])
+
+        def prep_w13_half(t_raw, codes, scales, g):
+            grouped = stage.tile([P, PASS * PACK], BF16, name="grouped_h", tag="grouped", align_bytes=64)
+            cast(
+                nc,
+                "A",
+                out=grouped[:].rearrange("p (t m j) -> p m j t", t=PACK, j=PACK),
+                in_=t_raw[:].rearrange("p j (m t) -> p m j t", t=PACK),
+            )
+            wc = slice(g * PASS, (g + 1) * PASS)
+            nc.vector.quantize_mx(out=codes[:, wc].bitcast(FP8X4), scales=scales[:, wc], in_=grouped[:])
 
         def prep_w2(t_raw, codes, scales, who, split):
             grouped = stage.tile([P, G * N * PACK], BF16, name="grouped2", tag="grouped", align_bytes=64)
@@ -229,13 +246,17 @@ def tile_routed_moe_kernel(tc, xT, w1, w3, w2, gate, offs, pos1, pos2, out):
             for m in range(M_TILES):
                 nc.scalar.copy(out=y_sb[m][:, e * C:(e + 1) * C], in_=acc[m])
 
-        for e in range(E):
+        for g in range(G):
+            prep_w13_half(loaded[("w1h%d" % g, 0)], w1q[0], w1s[0], g)
+            next_load()
+            prep_w13_half(loaded[("w3h%d" % g, 0)], w3q[0], w3s[0], g)
+            next_load()
+            layer1(0, g)
+        for e in range(1, E):
             prep_w13(loaded[("w1", e)], w1q[e], w1s[e], WHO_W1[e])
             next_load()
             prep_w13(loaded[("w3", e)], w3q[e], w3s[e], WHO_W3[e])
             next_load()
-            if e > 0:
-                gather(e)
             for g in range(G):
                 layer1(e, g)
         for e in range(E):

@@ -23,8 +23,8 @@ GELU = mybir.ActivationFunctionType.Gelu_apprx_tanh
 MULT = mybir.AluOpType.mult
 ADD = mybir.AluOpType.add
 
-WHO_W1 = (("A", "A"),) * 4
-WHO_W3 = (("A", "A"),) * 4
+WHO_W1 = (("A", "A"), ("S", "S"), ("S", "S"), ("A", "A"))
+WHO_W3 = (("A", "A"), ("V", "V"), ("V", "V"), ("A", "A"))
 WHO_W2 = (("A", "A"), ("A", "A"), ("A", "A"), ("V", "V"))
 LOOK = 4
 WINDOW = 2 * E * C

@@ -23,8 +23,8 @@ GELU = mybir.ActivationFunctionType.Gelu_apprx_tanh
 MULT = mybir.AluOpType.mult
 ADD = mybir.AluOpType.add
 
-WHO_W1 = (("A", "A"), ("S", "S"), ("S", "S"), ("A", "A"))
-WHO_W3 = (("A", "A"), ("V", "V"), ("V", "V"), ("A", "A"))
+WHO_W1 = (("A", "A"), ("S", "V"), ("S", "S"), ("S", "S"))
+WHO_W3 = (("A", "A"), ("V", "V"), ("V", "S"), ("V", "S"))
 WHO_W2 = (("A", "A"), ("A", "A"), ("A", "A"), ("V", "V"))
 LOOK = 4
 WINDOW = 2 * E * C
@@ -78,7 +78,7 @@ def tile_routed_moe_kernel(tc, xT, w1, w3, w2, gate, offs, pos1, pos2, out):
         y_sb = [keep.tile([P, E * C], F32, name="y_sb%d" % m) for m in range(M_TILES)]
         gate_t = [[keep.tile([P, T], F32, name="gate%d_%d" % (r, m)) for m in range(M_TILES)] for r in range(2)]
 
-        plan = [("x", 0)]
+        plan = [("x", 0), ("x", 1)]
         for g in range(G):
             plan.append(("w1h%d" % g, 0))
             plan.append(("w3h%d" % g, 0))
@@ -94,8 +94,8 @@ def tile_routed_moe_kernel(tc, xT, w1, w3, w2, gate, offs, pos1, pos2, out):
                 return
             kind, e = plan[i]
             if kind == "x":
-                t = raw.tile([P, PACK, T], F32, name="x_raw", tag="raw")
-                nc.sync.dma_start(out=t[:], in_=xT.rearrange("(p j) t -> p j t", j=PACK))
+                t = raw.tile([P, PACK, T // 2], F32, name="x_raw", tag="raw")
+                nc.sync.dma_start(out=t[:], in_=xT.rearrange("(p j) t -> p j t", j=PACK)[:, :, e * (T // 2):(e + 1) * (T // 2)])
             elif kind == "w2":
                 t = raw.tile([P, G, PACK, N], F32, name="w2_raw", tag="raw")
                 if e < E - 1:
@@ -119,9 +119,10 @@ def tile_routed_moe_kernel(tc, xT, w1, w3, w2, gate, offs, pos1, pos2, out):
                         nc.sync.dma_start(out=gate_t[r][m][:], in_=gate[r, m * P:(m + 1) * P, :])
 
         issue(0)
+        issue(1)
         nc.sync.dma_start(pos1_t[:], pos1)
         nc.sync.dma_start(pos2_t[:], pos2)
-        for i in range(1, LOOK + 1):
+        for i in range(2, LOOK + 1):
             issue(i)
         step = [LOOK + 1]
 
@@ -129,16 +130,17 @@ def tile_routed_moe_kernel(tc, xT, w1, w3, w2, gate, offs, pos1, pos2, out):
             issue(step[0])
             step[0] += 1
 
-        x_raw = loaded[("x", 0)]
-        xb = stage.tile([P, T * PACK], BF16, name="xb", tag="grouped", align_bytes=64)
-        for half, who in enumerate(("V", "S")):
+        for half in range(2):
+            xb = stage.tile([P, T // 2 * PACK], BF16, name="xb", tag="grouped", align_bytes=64)
             cast(
                 nc,
-                who,
-                out=xb[:, half * 1024:(half + 1) * 1024].rearrange("p (c i j) -> p c j i", i=4, j=PACK),
-                in_=x_raw[:, :, half * 256:(half + 1) * 256].rearrange("p j (c i) -> p c j i", i=4),
+                "V",
+                out=xb[:].rearrange("p (c i j) -> p c j i", i=4, j=PACK),
+                in_=loaded[("x", half)][:].rearrange("p j (c i) -> p c j i", i=4),
             )
-        nc.vector.quantize_mx(out=xq[:, 0:T].bitcast(FP8X4), scales=xs[:, 0:T], in_=xb[:])
+            next_load()
+            tc_cols = slice(half * (T // 2), (half + 1) * (T // 2))
+            nc.vector.quantize_mx(out=xq[:, tc_cols].bitcast(FP8X4), scales=xs[:, tc_cols], in_=xb[:])
         nc.vector.tensor_copy(out=xg_w[:], in_=xq[:].bitcast(U32).indirect(offs_t[:]))
         nc.vector.tensor_copy(out=xg_s[:], in_=xs[:].indirect(offs_t[:]))
 

@@ -150,8 +150,8 @@ def tile_routed_moe_kernel(tc, xT, w1, w3, w2, gate, offs, pos1, pos2, out):
                 cast(
                     nc,
                     who[g],
-                    out=grouped[:, g * PASS * PACK:(g + 1) * PASS * PACK].rearrange("p (t m j) -> p m j t", t=PACK, j=PACK),
-                    in_=t_raw[:, :, g * PASS:(g + 1) * PASS].rearrange("p j (m t) -> p m j t", t=PACK),
+                    out=grouped[:, g * PASS * PACK:(g + 1) * PASS * PACK].rearrange("p (t a b j) -> p a j t b", t=PACK, b=2, j=PACK),
+                    in_=t_raw[:, :, g * PASS:(g + 1) * PASS].rearrange("p j (a b t) -> p a j t b", b=2, t=PACK),
                 )
             nc.vector.quantize_mx(out=codes[:].bitcast(FP8X4), scales=scales[:], in_=grouped[:])
 
@@ -160,8 +160,8 @@ def tile_routed_moe_kernel(tc, xT, w1, w3, w2, gate, offs, pos1, pos2, out):
             cast(
                 nc,
                 "A",
-                out=grouped[:].rearrange("p (t m j) -> p m j t", t=PACK, j=PACK),
-                in_=t_raw[:].rearrange("p j (m t) -> p m j t", t=PACK),
+                out=grouped[:].rearrange("p (t a b j) -> p a j t b", t=PACK, b=2, j=PACK),
+                in_=t_raw[:].rearrange("p j (a b t) -> p a j t b", b=2, t=PACK),
             )
             wc = slice(g * PASS, (g + 1) * PASS)
             nc.vector.quantize_mx(out=codes[:, wc].bitcast(FP8X4), scales=scales[:, wc], in_=grouped[:])

@@ -216,9 +216,9 @@ def tile_routed_moe_kernel(tc, xT, w1, w3, w2, gate, offs, pos1, pos2, out):
                         stop=True,
                     )
                 nc.vector.tensor_tensor(
-                    out=hb[:, s * HALF * PACK:(s + 1) * HALF * PACK].rearrange("p (n j) -> p n j", j=PACK),
-                    in0=ga[:, :, s * HALF:(s + 1) * HALF].rearrange("p j n -> p n j"),
-                    in1=pb[:].rearrange("p j n -> p n j"),
+                    out=hb[:, s * HALF * PACK:(s + 1) * HALF * PACK].rearrange("p (c i j) -> p c j i", i=4, j=PACK),
+                    in0=ga[:, :, s * HALF:(s + 1) * HALF].rearrange("p j (c i) -> p c j i", i=4),
+                    in1=pb[:].rearrange("p j (c i) -> p c j i", i=4),
                     op=MULT,
                 )
             hc = slice(g * C, (g + 1) * C)

@@ -23,10 +23,12 @@ GELU = mybir.ActivationFunctionType.Gelu_apprx_tanh
 MULT = mybir.AluOpType.mult
 ADD = mybir.AluOpType.add
 
-WHO_W1 = (("A", "A"), ("S", "V"), ("S", "S"), ("S", "S"))
-WHO_W3 = (("A", "A"), ("V", "V"), ("V", "S"), ("V", "S"))
-WHO_W2 = (("A", "A"), ("A", "A"), ("A", "A"), ("V", "V"))
+PLAN = [("xw", 0, 0), ("w1", 0, 0), ("w3", 0, 0), ("w1", 0, 1), ("w3", 0, 1), ("w1", 1, -1), ("w3", 1, -1), ("w1", 2, -1), ("w3", 2, -1), ("w1", 3, -1), ("w3", 3, -1), ("w2", 0, -1), ("w2", 1, -1), ("w2", 2, -1), ("w2", 3, 0)]
+WHO = {("w1", 0, 0): "A", ("w1", 0, 1): "A", ("w3", 0, 0): "A", ("w3", 0, 1): "A", ("w1", 1, 0): "S", ("w1", 1, 1): "V", ("w3", 1, 0): "V", ("w3", 1, 1): "V", ("w1", 2, 0): "S", ("w1", 2, 1): "S", ("w3", 2, 0): "V", ("w3", 2, 1): "S", ("w1", 3, 0): "S", ("w1", 3, 1): "S", ("w3", 3, 0): "V", ("w3", 3, 1): "S", ("w2", 0, 0): "A", ("w2", 0, 1): "A", ("w2", 1, 0): "A", ("w2", 1, 1): "A", ("w2", 2, 0): "A", ("w2", 2, 1): "A", ("w2", 3, 0): "V", ("w2", 3, 1): "V"}
+Q_BY_PASS = ()
 LOOK = 4
+STAGE_BUFS = 3
+WORK_BUFS = 3
 WINDOW = 2 * E * C
 
 
@@ -45,8 +47,8 @@ def tile_routed_moe_kernel(tc, xT, w1, w3, w2, gate, offs, pos1, pos2, out):
         lists = ctx.enter_context(tc.tile_pool(name="lists", bufs=1))
         keep = ctx.enter_context(tc.tile_pool(name="keep", bufs=1))
         raw = ctx.enter_context(tc.tile_pool(name="raw", bufs=LOOK + 1))
-        stage = ctx.enter_context(tc.tile_pool(name="stage", bufs=3))
-        work = ctx.enter_context(tc.tile_pool(name="work", bufs=3))
+        stage = ctx.enter_context(tc.tile_pool(name="stage", bufs=STAGE_BUFS))
+        work = ctx.enter_context(tc.tile_pool(name="work", bufs=WORK_BUFS))
         psum = ctx.enter_context(tc.psum_pool(name="psum", bufs=3))
         psum_y = ctx.enter_context(tc.psum_pool(name="psum_y", bufs=2))
 
@@ -78,51 +80,45 @@ def tile_routed_moe_kernel(tc, xT, w1, w3, w2, gate, offs, pos1, pos2, out):
         y_sb = [keep.tile([P, E * C], F32, name="y_sb%d" % m) for m in range(M_TILES)]
         gate_t = [[keep.tile([P, T], F32, name="gate%d_%d" % (r, m)) for m in range(M_TILES)] for r in range(2)]
 
-        plan = [("x", 0), ("x", 1)]
-        for g in range(G):
-            plan.append(("w1h%d" % g, 0))
-            plan.append(("w3h%d" % g, 0))
-        for e in range(1, E):
-            plan.append(("w1", e))
-            plan.append(("w3", e))
-        for e in range(E):
-            plan.append(("w2", e))
         loaded = {}
 
         def issue(i):
-            if i >= len(plan):
+            if i >= len(PLAN):
                 return
-            kind, e = plan[i]
-            if kind == "x":
+            kind, e, part = PLAN[i]
+            if kind == "xw":
+                t = raw.tile([P, PACK, T], F32, name="xw_raw", tag="raw")
+                nc.sync.dma_start(out=t[:], in_=xT.rearrange("(p j) t -> p j t", j=PACK))
+            elif kind == "x":
                 t = raw.tile([P, PACK, T // 2], F32, name="x_raw", tag="raw")
                 nc.sync.dma_start(out=t[:], in_=xT.rearrange("(p j) t -> p j t", j=PACK)[:, :, e * (T // 2):(e + 1) * (T // 2)])
             elif kind == "w2":
                 t = raw.tile([P, G, PACK, N], F32, name="w2_raw", tag="raw")
-                if e < E - 1:
+                if part == -1:
                     nc.sync.dma_start(out=t[:], in_=w2[e].rearrange("(g p j) n -> p g j n", g=G, j=PACK))
                 else:
                     for g in range(G):
                         nc.sync.dma_start(out=t[:, g], in_=w2[e, g * PASS:(g + 1) * PASS, :].rearrange("(p j) n -> p j n", j=PACK))
-            elif len(kind) == 4:
-                src = w1 if kind[:2] == "w1" else w3
-                g = int(kind[3])
+            elif part >= 0:
+                src = w1 if kind == "w1" else w3
                 t = raw.tile([P, PACK, PASS], F32, name="w13h_raw", tag="raw")
-                nc.sync.dma_start(out=t[:], in_=src[e, :, g * PASS:(g + 1) * PASS].rearrange("(p j) h -> p j h", j=PACK))
+                nc.sync.dma_start(out=t[:], in_=src[e, :, part * PASS:(part + 1) * PASS].rearrange("(p j) h -> p j h", j=PACK))
             else:
                 src = w1 if kind == "w1" else w3
                 t = raw.tile([P, PACK, H], F32, name="w13_raw", tag="raw")
                 nc.sync.dma_start(out=t[:], in_=src[e].rearrange("(p j) h -> p j h", j=PACK))
-            loaded[(kind, e)] = t
-            if i == len(plan) - 1:
+            loaded[PLAN[i]] = t
+            if i == len(PLAN) - 1:
+                nc.sync.dma_start(pos1_t[:], pos1)
+                nc.sync.dma_start(pos2_t[:], pos2)
                 for m in range(M_TILES):
                     for r in range(2):
                         nc.sync.dma_start(out=gate_t[r][m][:], in_=gate[r, m * P:(m + 1) * P, :])
 
-        issue(0)
-        issue(1)
-        nc.sync.dma_start(pos1_t[:], pos1)
-        nc.sync.dma_start(pos2_t[:], pos2)
-        for i in range(2, LOOK + 1):
+        n_x = len([item for item in PLAN if item[0] in ("x", "xw")])
+        for i in range(n_x):
+            issue(i)
+        for i in range(n_x, LOOK + 1):
             issue(i)
         step = [LOOK + 1]
 
@@ -130,48 +126,66 @@ def tile_routed_moe_kernel(tc, xT, w1, w3, w2, gate, offs, pos1, pos2, out):
             issue(step[0])
             step[0] += 1
 
-        for half in range(2):
+        def prep_x(half):
             xb = stage.tile([P, T // 2 * PACK], BF16, name="xb", tag="grouped", align_bytes=64)
             cast(
                 nc,
                 "V",
                 out=xb[:].rearrange("p (c i j) -> p c j i", i=4, j=PACK),
-                in_=loaded[("x", half)][:].rearrange("p j (c i) -> p c j i", i=4),
+                in_=loaded[("x", half, 0)][:].rearrange("p j (c i) -> p c j i", i=4),
             )
             next_load()
             tc_cols = slice(half * (T // 2), (half + 1) * (T // 2))
             nc.vector.quantize_mx(out=xq[:, tc_cols].bitcast(FP8X4), scales=xs[:, tc_cols], in_=xb[:])
-        nc.vector.tensor_copy(out=xg_w[:], in_=xq[:].bitcast(U32).indirect(offs_t[:]))
-        nc.vector.tensor_copy(out=xg_s[:], in_=xs[:].indirect(offs_t[:]))
+            if half == 1:
+                nc.vector.tensor_copy(out=xg_w[:], in_=xq[:].bitcast(U32).indirect(offs_t[:]))
+                nc.vector.tensor_copy(out=xg_s[:], in_=xs[:].indirect(offs_t[:]))
 
-        def prep_w13(t_raw, codes, scales, who):
+        def prep_x_whole():
+            xb = stage.tile([P, T * PACK], BF16, name="xbw", tag="grouped", align_bytes=64)
+            cast(
+                nc,
+                "V",
+                out=xb[:].rearrange("p (c i j) -> p c j i", i=4, j=PACK),
+                in_=loaded[("xw", 0, 0)][:].rearrange("p j (c i) -> p c j i", i=4),
+            )
+            next_load()
+            nc.vector.quantize_mx(out=xq[:, :T].bitcast(FP8X4), scales=xs[:, :T], in_=xb[:])
+            nc.vector.tensor_copy(out=xg_w[:], in_=xq[:].bitcast(U32).indirect(offs_t[:]))
+            nc.vector.tensor_copy(out=xg_s[:], in_=xs[:].indirect(offs_t[:]))
+
+        def prep_w13(kind, e, t_raw, codes, scales):
             grouped = stage.tile([P, H * PACK], BF16, name="grouped", tag="grouped", align_bytes=64)
             for g in range(G):
                 cast(
                     nc,
-                    who[g],
+                    WHO[(kind, e, g)],
                     out=grouped[:, g * PASS * PACK:(g + 1) * PASS * PACK].rearrange("p (t a b j) -> p a j t b", t=PACK, b=2, j=PACK),
                     in_=t_raw[:, :, g * PASS:(g + 1) * PASS].rearrange("p j (a b t) -> p a j t b", b=2, t=PACK),
                 )
-            nc.vector.quantize_mx(out=codes[:].bitcast(FP8X4), scales=scales[:], in_=grouped[:])
+                if (kind, e) in Q_BY_PASS:
+                    wc = slice(g * PASS, (g + 1) * PASS)
+                    nc.vector.quantize_mx(out=codes[:, wc].bitcast(FP8X4), scales=scales[:, wc], in_=grouped[:, g * PASS * PACK:(g + 1) * PASS * PACK])
+            if (kind, e) not in Q_BY_PASS:
+                nc.vector.quantize_mx(out=codes[:].bitcast(FP8X4), scales=scales[:], in_=grouped[:])
 
-        def prep_w13_half(t_raw, codes, scales, g):
+        def prep_w13_half(kind, e, g, t_raw, codes, scales):
             grouped = stage.tile([P, PASS * PACK], BF16, name="grouped_h", tag="grouped", align_bytes=64)
             cast(
                 nc,
-                "A",
+                WHO[(kind, e, g)],
                 out=grouped[:].rearrange("p (t a b j) -> p a j t b", t=PACK, b=2, j=PACK),
                 in_=t_raw[:].rearrange("p j (a b t) -> p a j t b", b=2, t=PACK),
             )
             wc = slice(g * PASS, (g + 1) * PASS)
             nc.vector.quantize_mx(out=codes[:, wc].bitcast(FP8X4), scales=scales[:, wc], in_=grouped[:])
 
-        def prep_w2(t_raw, codes, scales, who, split):
+        def prep_w2(e, t_raw, codes, scales, split):
             grouped = stage.tile([P, G * N * PACK], BF16, name="grouped2", tag="grouped", align_bytes=64)
             for g in range(G):
                 cast(
                     nc,
-                    who[g],
+                    WHO[("w2", e, g)],
                     out=grouped[:, g * N * PACK:(g + 1) * N * PACK].rearrange("p (c i j) -> p c j i", i=4, j=PACK),
                     in_=t_raw[:, g, :, :].rearrange("p j (c i) -> p c j i", i=4),
                 )
@@ -224,8 +238,8 @@ def tile_routed_moe_kernel(tc, xT, w1, w3, w2, gate, offs, pos1, pos2, out):
             hc = slice(g * C, (g + 1) * C)
             nc.vector.quantize_mx(out=hq[e][:, hc].bitcast(FP8X4), scales=hs[e][:, hc], in_=hb[:])
 
-        def layer2(e):
-            if e < E - 1:
+        def layer2(e, last):
+            if not last:
                 py = psum_y.tile([P, M_TILES, C], F32, name="py", tag="py")
                 acc = [py[:, m, :] for m in range(M_TILES)]
                 order = [(m, g) for m in range(M_TILES) for g in range(G)]
@@ -233,38 +247,53 @@ def tile_routed_moe_kernel(tc, xT, w1, w3, w2, gate, offs, pos1, pos2, out):
                 acc = [psum_y.tile([P, C], F32, name="py%d" % m, tag="py")[:] for m in range(M_TILES)]
                 order = [(m, g) for g in range(G) for m in range(M_TILES)]
             for m, g in order:
-                if True:
-                    wc = slice(g * N + m * P, g * N + (m + 1) * P)
-                    hc = slice(g * C, (g + 1) * C)
-                    nc.tensor.matmul_mx(
-                        out=acc[m],
-                        lhsT=w2q[e][:, wc].bitcast(FP8X4),
-                        lhsT_scale=w2s[e][:, wc],
-                        rhs=hq[e][:, hc].bitcast(FP8X4),
-                        rhs_scale=hs[e][:, hc],
-                        start=(g == 0),
-                        stop=(g == G - 1),
-                    )
+                wc = slice(g * N + m * P, g * N + (m + 1) * P)
+                hc = slice(g * C, (g + 1) * C)
+                nc.tensor.matmul_mx(
+                    out=acc[m],
+                    lhsT=w2q[e][:, wc].bitcast(FP8X4),
+                    lhsT_scale=w2s[e][:, wc],
+                    rhs=hq[e][:, hc].bitcast(FP8X4),
+                    rhs_scale=hs[e][:, hc],
+                    start=(g == 0),
+                    stop=(g == G - 1),
+                )
             for m in range(M_TILES):
                 nc.scalar.copy(out=y_sb[m][:, e * C:(e + 1) * C], in_=acc[m])
 
-        for g in range(G):
-            prep_w13_half(loaded[("w1h%d" % g, 0)], w1q[0], w1s[0], g)
+        have = set()
+        done1 = set()
+        done2 = []
+        for item in PLAN:
+            kind, e, part = item
+            if kind == "xw":
+                prep_x_whole()
+                continue
+            if kind == "x":
+                prep_x(e)
+                continue
+            if kind == "w2":
+                prep_w2(e, loaded[item], w2q[e], w2s[e], part != -1)
+                have.add(("w2", e))
+            else:
+                codes, scales = (w1q[e], w1s[e]) if kind == "w1" else (w3q[e], w3s[e])
+                if part == -1:
+                    prep_w13(kind, e, loaded[item], codes, scales)
+                    for g in range(G):
+                        have.add((kind, e, g))
+                else:
+                    prep_w13_half(kind, e, part, loaded[item], codes, scales)
+                    have.add((kind, e, part))
             next_load()
-            prep_w13_half(loaded[("w3h%d" % g, 0)], w3q[0], w3s[0], g)
-            next_load()
-            layer1(0, g)
-        for e in range(1, E):
-            prep_w13(loaded[("w1", e)], w1q[e], w1s[e], WHO_W1[e])
-            next_load()
-            prep_w13(loaded[("w3", e)], w3q[e], w3s[e], WHO_W3[e])
-            next_load()
-            for g in range(G):
-                layer1(e, g)
-        for e in range(E):
-            prep_w2(loaded[("w2", e)], w2q[e], w2s[e], WHO_W2[e], e == E - 1)
-            next_load()
-            layer2(e)
+            for ee in range(E):
+                for g in range(G):
+                    if ("w1", ee, g) in have and ("w3", ee, g) in have and (ee, g) not in done1:
+                        layer1(ee, g)
+                        done1.add((ee, g))
+            for ee in range(E):
+                if ("w2", ee) in have and ee not in done2 and all((ee, g) in done1 for g in range(G)):
+                    layer2(ee, len(done2) == E - 1)
+                    done2.append(ee)
 
         for m in range(M_TILES):
             o1 = work.tile([P, T], F32, name="o1", tag="o1")

@@ -1,6 +1,7 @@
 from contextlib import ExitStack
 
 import concourse.mybir as mybir
+from concourse.masks import make_identity
 
 FLOPS = 2 * 1024 * (2 * 512 * 1024 + 1024 * 256)
 
@@ -61,6 +62,9 @@ def tile_routed_moe_kernel(tc, xT, w1, w3, w2, gate, offs, pos1, pos2, out):
         warm_out = keep.tile([P, 1], F32, name="warm_out")
         nc.vector.memset(warm[:], 0.0)
         nc.scalar.activation(out=warm_out[:], in_=warm[:], func=GELU)
+
+        ident = keep.tile([P, P], F32, name="ident")
+        make_identity(nc, ident[:])
 
         xq = keep.tile([P, WINDOW], I32, name="xq", align_bytes=64)
         xs = keep.tile([P, WINDOW], U8, name="xs", align_bytes=64)
@@ -301,5 +305,14 @@ def tile_routed_moe_kernel(tc, xT, w1, w3, w2, gate, offs, pos1, pos2, out):
             o = work.tile([P, T], F32, name="o", tag="o")
             nc.vector.tensor_tensor(out=o1[:], in0=y_sb[m][:].indirect(pos1_t[:]), in1=gate_t[0][m][:], op=MULT)
             nc.vector.tensor_tensor(out=o2[:], in0=y_sb[m][:].indirect(pos2_t[:]), in1=gate_t[1][m][:], op=MULT)
-            nc.vector.tensor_tensor(out=o[:], in0=o1[:], in1=o2[:], op=ADD)
-            nc.sync.dma_start(out=out[m * P:(m + 1) * P, :], in_=o[:])
+            if m == 0:
+                po = psum_y.tile([P, T], F32, name="po", tag="py")
+                nc.tensor.matmul(out=po[:], lhsT=ident[:], rhs=o1[:], start=True, stop=False)
+                nc.tensor.matmul(out=po[:], lhsT=ident[:], rhs=o2[:], start=False, stop=True)
+                nc.scalar.copy(out=o[:], in_=po[:])
+            else:
+                nc.vector.tensor_tensor(out=o[:], in0=o1[:], in1=o2[:], op=ADD)
+            if m == 0:
+                nc.scalar.dma_start(out=out[m * P:(m + 1) * P, :], in_=o[:])
+            else:
+                nc.sync.dma_start(out=out[m * P:(m + 1) * P, :], in_=o[:])

from contextlib import ExitStack

import concourse.mybir as mybir
from concourse.masks import make_identity

FLOPS = 2 * 1024 * (2 * 512 * 1024 + 1024 * 256)

K, T, E, C, H, N = 512, 512, 4, 256, 1024, 256
P = 128
PACK = 4
PASS = P * PACK
G = H // PASS
HALF = 128
M_TILES = N // P

F32 = mybir.dt.float32
BF16 = mybir.dt.bfloat16
U32 = mybir.dt.uint32
I32 = mybir.dt.int32
U16 = mybir.dt.uint16
U8 = mybir.dt.uint8
FP8X4 = mybir.dt.float8_e4m3fn_x4
GELU = mybir.ActivationFunctionType.Gelu_apprx_tanh
MULT = mybir.AluOpType.mult
ADD = mybir.AluOpType.add

PLAN = [("xw", 0, 0), ("w1", 0, 0), ("w3", 0, 0), ("w1", 0, 1), ("w3", 0, 1), ("w1", 1, -1), ("w3", 1, -1), ("w1", 2, -1), ("w3", 2, -1), ("w1", 3, -1), ("w3", 3, -1), ("w2", 0, -1), ("w2", 1, -1), ("w2", 2, -1), ("w2", 3, 0)]
WHO = {("w1", 0, 0): "A", ("w1", 0, 1): "A", ("w3", 0, 0): "A", ("w3", 0, 1): "A", ("w1", 1, 0): "S", ("w1", 1, 1): "V", ("w3", 1, 0): "V", ("w3", 1, 1): "V", ("w1", 2, 0): "S", ("w1", 2, 1): "S", ("w3", 2, 0): "V", ("w3", 2, 1): "S", ("w1", 3, 0): "S", ("w1", 3, 1): "S", ("w3", 3, 0): "V", ("w3", 3, 1): "S", ("w2", 0, 0): "A", ("w2", 0, 1): "A", ("w2", 1, 0): "A", ("w2", 1, 1): "A", ("w2", 2, 0): "A", ("w2", 2, 1): "A", ("w2", 3, 0): "V", ("w2", 3, 1): "V"}
Q_BY_PASS = ()
LOOK = 4
STAGE_BUFS = 3
WORK_BUFS = 3
WINDOW = 2 * E * C


def cast(nc, who, out, in_):
    if who == "A":
        nc.any.tensor_copy(out=out, in_=in_)
    elif who == "V":
        nc.vector.tensor_copy(out=out, in_=in_)
    else:
        nc.scalar.copy(out=out, in_=in_)


def tile_routed_moe_kernel(tc, xT, w1, w3, w2, gate, offs, pos1, pos2, out):
    nc = tc.nc
    with ExitStack() as ctx:
        lists = ctx.enter_context(tc.tile_pool(name="lists", bufs=1))
        keep = ctx.enter_context(tc.tile_pool(name="keep", bufs=1))
        raw = ctx.enter_context(tc.tile_pool(name="raw", bufs=LOOK + 1))
        stage = ctx.enter_context(tc.tile_pool(name="stage", bufs=STAGE_BUFS))
        work = ctx.enter_context(tc.tile_pool(name="work", bufs=WORK_BUFS))
        psum = ctx.enter_context(tc.psum_pool(name="psum", bufs=3))
        psum_y = ctx.enter_context(tc.psum_pool(name="psum_y", bufs=2))

        offs_t = lists.tile([P, E * C // 16], U16, name="offs_t")
        pos1_t = lists.tile([P, T // 16], U16, name="pos1_t")
        pos2_t = lists.tile([P, T // 16], U16, name="pos2_t")
        nc.sync.dma_start(offs_t[:], offs)

        warm = keep.tile([P, 1], F32, name="warm")
        warm_out = keep.tile([P, 1], F32, name="warm_out")
        nc.vector.memset(warm[:], 0.0)
        nc.scalar.activation(out=warm_out[:], in_=warm[:], func=GELU)

        ident = keep.tile([P, P], F32, name="ident")
        make_identity(nc, ident[:])

        xq = keep.tile([P, WINDOW], I32, name="xq", align_bytes=64)
        xs = keep.tile([P, WINDOW], U8, name="xs", align_bytes=64)
        xg_w = keep.tile([P, E * C], U32, name="xg_w", align_bytes=64)
        xg_s = keep.tile([P, E * C], U8, name="xg_s", align_bytes=64)
        nc.gpsimd.memset(xs[:], 0)
        nc.vector.memset(xq[:, T:], 0)

        w1q = [keep.tile([P, H], U32, name="w1q%d" % e, align_bytes=64) for e in range(E)]
        w1s = [keep.tile([P, H], U8, name="w1s%d" % e, align_bytes=64) for e in range(E)]
        w3q = [keep.tile([P, H], U32, name="w3q%d" % e, align_bytes=64) for e in range(E)]
        w3s = [keep.tile([P, H], U8, name="w3s%d" % e, align_bytes=64) for e in range(E)]
        w2q = [keep.tile([P, G * N], U32, name="w2q%d" % e, align_bytes=64) for e in range(E)]
        w2s = [keep.tile([P, G * N], U8, name="w2s%d" % e, align_bytes=64) for e in range(E)]
        hq = [keep.tile([P, G * C], U32, name="hq%d" % e, align_bytes=64) for e in range(E)]
        hs = [keep.tile([P, G * C], U8, name="hs%d" % e, align_bytes=64) for e in range(E)]
        y_sb = [keep.tile([P, E * C], F32, name="y_sb%d" % m) for m in range(M_TILES)]
        gate_t = [[keep.tile([P, T], F32, name="gate%d_%d" % (r, m)) for m in range(M_TILES)] for r in range(2)]

        loaded = {}

        def issue(i):
            if i >= len(PLAN):
                return
            kind, e, part = PLAN[i]
            if kind == "xw":
                t = raw.tile([P, PACK, T], F32, name="xw_raw", tag="raw")
                nc.sync.dma_start(out=t[:], in_=xT.rearrange("(p j) t -> p j t", j=PACK))
            elif kind == "x":
                t = raw.tile([P, PACK, T // 2], F32, name="x_raw", tag="raw")
                nc.sync.dma_start(out=t[:], in_=xT.rearrange("(p j) t -> p j t", j=PACK)[:, :, e * (T // 2):(e + 1) * (T // 2)])
            elif kind == "w2":
                t = raw.tile([P, G, PACK, N], F32, name="w2_raw", tag="raw")
                if part == -1:
                    nc.sync.dma_start(out=t[:], in_=w2[e].rearrange("(g p j) n -> p g j n", g=G, j=PACK))
                else:
                    for g in range(G):
                        nc.sync.dma_start(out=t[:, g], in_=w2[e, g * PASS:(g + 1) * PASS, :].rearrange("(p j) n -> p j n", j=PACK))
            elif part >= 0:
                src = w1 if kind == "w1" else w3
                t = raw.tile([P, PACK, PASS], F32, name="w13h_raw", tag="raw")
                nc.sync.dma_start(out=t[:], in_=src[e, :, part * PASS:(part + 1) * PASS].rearrange("(p j) h -> p j h", j=PACK))
            else:
                src = w1 if kind == "w1" else w3
                t = raw.tile([P, PACK, H], F32, name="w13_raw", tag="raw")
                nc.sync.dma_start(out=t[:], in_=src[e].rearrange("(p j) h -> p j h", j=PACK))
            loaded[PLAN[i]] = t
            if i == len(PLAN) - 1:
                nc.sync.dma_start(pos1_t[:], pos1)
                nc.sync.dma_start(pos2_t[:], pos2)
                for m in range(M_TILES):
                    for r in range(2):
                        nc.sync.dma_start(out=gate_t[r][m][:], in_=gate[r, m * P:(m + 1) * P, :])

        n_x = len([item for item in PLAN if item[0] in ("x", "xw")])
        for i in range(n_x):
            issue(i)
        for i in range(n_x, LOOK + 1):
            issue(i)
        step = [LOOK + 1]

        def next_load():
            issue(step[0])
            step[0] += 1

        def prep_x(half):
            xb = stage.tile([P, T // 2 * PACK], BF16, name="xb", tag="grouped", align_bytes=64)
            cast(
                nc,
                "V",
                out=xb[:].rearrange("p (c i j) -> p c j i", i=4, j=PACK),
                in_=loaded[("x", half, 0)][:].rearrange("p j (c i) -> p c j i", i=4),
            )
            next_load()
            tc_cols = slice(half * (T // 2), (half + 1) * (T // 2))
            nc.vector.quantize_mx(out=xq[:, tc_cols].bitcast(FP8X4), scales=xs[:, tc_cols], in_=xb[:])
            if half == 1:
                nc.vector.tensor_copy(out=xg_w[:], in_=xq[:].bitcast(U32).indirect(offs_t[:]))
                nc.vector.tensor_copy(out=xg_s[:], in_=xs[:].indirect(offs_t[:]))

        def prep_x_whole():
            xb = stage.tile([P, T * PACK], BF16, name="xbw", tag="grouped", align_bytes=64)
            cast(
                nc,
                "V",
                out=xb[:].rearrange("p (c i j) -> p c j i", i=4, j=PACK),
                in_=loaded[("xw", 0, 0)][:].rearrange("p j (c i) -> p c j i", i=4),
            )
            next_load()
            nc.vector.quantize_mx(out=xq[:, :T].bitcast(FP8X4), scales=xs[:, :T], in_=xb[:])
            nc.vector.tensor_copy(out=xg_w[:], in_=xq[:].bitcast(U32).indirect(offs_t[:]))
            nc.vector.tensor_copy(out=xg_s[:], in_=xs[:].indirect(offs_t[:]))

        def prep_w13(kind, e, t_raw, codes, scales):
            grouped = stage.tile([P, H * PACK], BF16, name="grouped", tag="grouped", align_bytes=64)
            for g in range(G):
                cast(
                    nc,
                    WHO[(kind, e, g)],
                    out=grouped[:, g * PASS * PACK:(g + 1) * PASS * PACK].rearrange("p (t a b j) -> p a j t b", t=PACK, b=2, j=PACK),
                    in_=t_raw[:, :, g * PASS:(g + 1) * PASS].rearrange("p j (a b t) -> p a j t b", b=2, t=PACK),
                )
                if (kind, e) in Q_BY_PASS:
                    wc = slice(g * PASS, (g + 1) * PASS)
                    nc.vector.quantize_mx(out=codes[:, wc].bitcast(FP8X4), scales=scales[:, wc], in_=grouped[:, g * PASS * PACK:(g + 1) * PASS * PACK])
            if (kind, e) not in Q_BY_PASS:
                nc.vector.quantize_mx(out=codes[:].bitcast(FP8X4), scales=scales[:], in_=grouped[:])

        def prep_w13_half(kind, e, g, t_raw, codes, scales):
            grouped = stage.tile([P, PASS * PACK], BF16, name="grouped_h", tag="grouped", align_bytes=64)
            cast(
                nc,
                WHO[(kind, e, g)],
                out=grouped[:].rearrange("p (t a b j) -> p a j t b", t=PACK, b=2, j=PACK),
                in_=t_raw[:].rearrange("p j (a b t) -> p a j t b", b=2, t=PACK),
            )
            wc = slice(g * PASS, (g + 1) * PASS)
            nc.vector.quantize_mx(out=codes[:, wc].bitcast(FP8X4), scales=scales[:, wc], in_=grouped[:])

        def prep_w2(e, t_raw, codes, scales, split):
            grouped = stage.tile([P, G * N * PACK], BF16, name="grouped2", tag="grouped", align_bytes=64)
            for g in range(G):
                cast(
                    nc,
                    WHO[("w2", e, g)],
                    out=grouped[:, g * N * PACK:(g + 1) * N * PACK].rearrange("p (c i j) -> p c j i", i=4, j=PACK),
                    in_=t_raw[:, g, :, :].rearrange("p j (c i) -> p c j i", i=4),
                )
                if split:
                    wc = slice(g * N, (g + 1) * N)
                    nc.vector.quantize_mx(
                        out=codes[:, wc].bitcast(FP8X4), scales=scales[:, wc], in_=grouped[:, g * N * PACK:(g + 1) * N * PACK]
                    )
            if not split:
                nc.vector.quantize_mx(out=codes[:].bitcast(FP8X4), scales=scales[:], in_=grouped[:])

        def layer1(e, g):
            hb = work.tile([P, C * PACK], BF16, name="hb", tag="hb", align_bytes=64)
            ga = work.tile([P, PACK, C], F32, name="ga", tag="ga")
            for u in range(2):
                pa = psum.tile([P, 2, C], F32, name="pa", tag="pa")
                for v in range(2):
                    t = 2 * u + v
                    wc = slice(g * PASS + t * P, g * PASS + (t + 1) * P)
                    nc.tensor.matmul_mx(
                        out=pa[:, v, :],
                        lhsT=w1q[e][:, wc].bitcast(FP8X4),
                        lhsT_scale=w1s[e][:, wc],
                        rhs=xg_w[:, e * C:(e + 1) * C].bitcast(FP8X4),
                        rhs_scale=xg_s[:, e * C:(e + 1) * C],
                        start=True,
                        stop=True,
                    )
                nc.scalar.activation(out=ga[:, 2 * u:2 * u + 2, :], in_=pa[:], func=GELU)
            for s in range(C // HALF):
                cols = slice(e * C + s * HALF, e * C + (s + 1) * HALF)
                pb = psum.tile([P, PACK, HALF], F32, name="pb", tag="pb")
                for t in range(PACK):
                    wc = slice(g * PASS + t * P, g * PASS + (t + 1) * P)
                    nc.tensor.matmul_mx(
                        out=pb[:, t, :],
                        lhsT=w3q[e][:, wc].bitcast(FP8X4),
                        lhsT_scale=w3s[e][:, wc],
                        rhs=xg_w[:, cols].bitcast(FP8X4),
                        rhs_scale=xg_s[:, cols],
                        start=True,
                        stop=True,
                    )
                nc.vector.tensor_tensor(
                    out=hb[:, s * HALF * PACK:(s + 1) * HALF * PACK].rearrange("p (c i j) -> p c j i", i=4, j=PACK),
                    in0=ga[:, :, s * HALF:(s + 1) * HALF].rearrange("p j (c i) -> p c j i", i=4),
                    in1=pb[:].rearrange("p j (c i) -> p c j i", i=4),
                    op=MULT,
                )
            hc = slice(g * C, (g + 1) * C)
            nc.vector.quantize_mx(out=hq[e][:, hc].bitcast(FP8X4), scales=hs[e][:, hc], in_=hb[:])

        def layer2(e, last):
            if not last:
                py = psum_y.tile([P, M_TILES, C], F32, name="py", tag="py")
                acc = [py[:, m, :] for m in range(M_TILES)]
                order = [(m, g) for m in range(M_TILES) for g in range(G)]
            else:
                acc = [psum_y.tile([P, C], F32, name="py%d" % m, tag="py")[:] for m in range(M_TILES)]
                order = [(m, g) for g in range(G) for m in range(M_TILES)]
            for m, g in order:
                wc = slice(g * N + m * P, g * N + (m + 1) * P)
                hc = slice(g * C, (g + 1) * C)
                nc.tensor.matmul_mx(
                    out=acc[m],
                    lhsT=w2q[e][:, wc].bitcast(FP8X4),
                    lhsT_scale=w2s[e][:, wc],
                    rhs=hq[e][:, hc].bitcast(FP8X4),
                    rhs_scale=hs[e][:, hc],
                    start=(g == 0),
                    stop=(g == G - 1),
                )
            for m in range(M_TILES):
                nc.scalar.copy(out=y_sb[m][:, e * C:(e + 1) * C], in_=acc[m])

        have = set()
        done1 = set()
        done2 = []
        for item in PLAN:
            kind, e, part = item
            if kind == "xw":
                prep_x_whole()
                continue
            if kind == "x":
                prep_x(e)
                continue
            if kind == "w2":
                prep_w2(e, loaded[item], w2q[e], w2s[e], part != -1)
                have.add(("w2", e))
            else:
                codes, scales = (w1q[e], w1s[e]) if kind == "w1" else (w3q[e], w3s[e])
                if part == -1:
                    prep_w13(kind, e, loaded[item], codes, scales)
                    for g in range(G):
                        have.add((kind, e, g))
                else:
                    prep_w13_half(kind, e, part, loaded[item], codes, scales)
                    have.add((kind, e, part))
            next_load()
            for ee in range(E):
                for g in range(G):
                    if ("w1", ee, g) in have and ("w3", ee, g) in have and (ee, g) not in done1:
                        layer1(ee, g)
                        done1.add((ee, g))
            for ee in range(E):
                if ("w2", ee) in have and ee not in done2 and all((ee, g) in done1 for g in range(G)):
                    layer2(ee, len(done2) == E - 1)
                    done2.append(ee)

        for m in range(M_TILES):
            o1 = work.tile([P, T], F32, name="o1", tag="o1")
            o2 = work.tile([P, T], F32, name="o2", tag="o2")
            o = work.tile([P, T], F32, name="o", tag="o")
            nc.vector.tensor_tensor(out=o1[:], in0=y_sb[m][:].indirect(pos1_t[:]), in1=gate_t[0][m][:], op=MULT)
            nc.vector.tensor_tensor(out=o2[:], in0=y_sb[m][:].indirect(pos2_t[:]), in1=gate_t[1][m][:], op=MULT)
            if m == 0:
                po = psum_y.tile([P, T], F32, name="po", tag="py")
                nc.tensor.matmul(out=po[:], lhsT=ident[:], rhs=o1[:], start=True, stop=False)
                nc.tensor.matmul(out=po[:], lhsT=ident[:], rhs=o2[:], start=False, stop=True)
                nc.scalar.copy(out=o[:], in_=po[:])
            else:
                nc.vector.tensor_tensor(out=o[:], in0=o1[:], in1=o2[:], op=ADD)
            if m == 0:
                nc.scalar.dma_start(out=out[m * P:(m + 1) * P, :], in_=o[:])
            else:
                nc.sync.dma_start(out=out[m * P:(m + 1) * P, :], in_=o[:])
